import numpy as np
import ml_dtypes


def mxq(x, axis, fmt="e4m3"):
    dtype, down = {"e4m3": (ml_dtypes.float8_e4m3fn, 7), "e5m2": (ml_dtypes.float8_e5m2, 14)}[fmt]
    v = np.moveaxis(np.asarray(x, np.float32).astype(ml_dtypes.bfloat16).astype(np.float64), axis, -1)
    blocks = v.reshape(v.shape[:-1] + (-1, 32))
    amax = np.abs(blocks).max(-1, keepdims=True)
    byte = np.maximum(np.where(amax > 0, np.frexp(amax)[1] - 1 + 127, 0) - down, 1)
    scale = np.exp2(byte - 127.0)
    codes = (blocks / scale).astype(np.float32).astype(dtype).astype(np.float64)
    return np.moveaxis((codes * scale).reshape(v.shape), -1, axis)


WIDE = False


def mx_kscale(k):
    if not WIDE:
        return np.ones(k)
    levels = np.array([10, -10, 5, -5, 0])
    if k % 512:
        return np.exp2(np.random.permutation(np.resize(levels, k // 32))).repeat(32)
    a = np.empty((k // 512, 16))
    for p in range(k // 512):
        a[p, :8] = np.random.permutation(np.resize(levels, 8))
        for g in range(8):
            far = levels[np.abs(levels - a[p, g]) >= 10]
            a[p, g + 8] = far[np.random.randint(len(far))]
    return np.exp2(a.ravel()).repeat(32)


def f64(x):
    return np.asarray(x).astype(np.float64)


def striped(idx):
    return np.tile(idx.reshape(-1, 16).T, (8, 1)).astype(np.uint16)


def unstriped(offs):
    return offs[:16].T.reshape(-1).astype(np.int64)


E2M1 = np.array([0.0, 0.5, 1.0, 1.5, 2.0, 3.0, 4.0, 6.0, -0.0, -0.5, -1.0, -1.5, -2.0, -3.0, -4.0, -6.0])


def pack_weight(w, fmt):
    k, n = w.shape
    w = f64(np.asarray(w, np.float32).astype(ml_dtypes.bfloat16)).reshape(k // 32, 32, n)
    amax = np.abs(w).max(1)
    if fmt == "e4m3":
        byte = np.frexp(amax)[1] - 1 + 127 - 7
    else:
        mant, ex = np.frexp(amax / 6.0)
        byte = np.where(mant > 0.5, ex, ex - 1) + 127
    byte = np.clip(np.where(amax > 0, byte, 1), 1, 254)
    scaled = (w * np.exp2(127.0 - byte)[:, None, :]).reshape(k, n).astype(np.float32)
    by_word = np.ascontiguousarray(scaled.reshape(k // 512, 128, 4, n).transpose(0, 1, 3, 2))
    if fmt == "e4m3":
        words = by_word.astype(ml_dtypes.float8_e4m3fn).view(np.uint8)
    else:
        c = by_word.astype(ml_dtypes.float4_e2m1fn).view(np.uint8) & 0xF
        words = (c[..., 0::2] | (c[..., 1::2] << 4)).reshape(k // 512, 128, 2 * n)
    return np.ascontiguousarray(words), np.ascontiguousarray(byte.astype(np.uint8).reshape(k // 512, 16, n))


def unpack_weight(words, scales, fmt):
    g, _, n = scales.shape
    words = np.ascontiguousarray(words).reshape(g, 128, n, -1)
    if fmt == "e4m3":
        vals = words.view(ml_dtypes.float8_e4m3fn).astype(np.float64)
    else:
        nib = np.empty((g, 128, n, 4), np.uint8)
        nib[..., 0::2] = words & 0xF
        nib[..., 1::2] = words >> 4
        vals = E2M1[nib]
    vals = vals * np.repeat(np.exp2(scales.astype(np.float64) - 127.0), 8, axis=1)[..., None]
    return vals.transpose(0, 1, 3, 2).reshape(g * 512, n)


def gelu(v):
    return 0.5 * v * (1.0 + np.tanh(np.sqrt(2.0 / np.pi) * (v + 0.044715 * v**3)))


def striped8(idx):
    return np.concatenate([v.reshape(-1, 16).T for v in idx]).astype(np.uint16)


def unstriped8(offs):
    return np.stack([offs[16 * g:16 * g + 16].T.reshape(-1) for g in range(8)]).astype(np.int64)


def heads(h, wgt, idx8):
    r = np.arange(h.shape[0])
    return wgt[r // 4 % 128] * h[r[:, None], idx8[r % 512 // 64]]


K, T, S, H, P, N = 1024, 4096, 1024, 1024, 512, 512

def setup_inputs():
    n = np.random.standard_normal
    s = mx_kscale(K)[:, None]
    u = mx_kscale(H)[:, None]
    tab_words, tab_scales = pack_weight(n((K, T)) * s, "e4m3")
    w4_words, w4_scales = pack_weight(1.5 * n((H, N)) / np.sqrt(H) / u, "e2m1")
    offs = striped(np.random.permutation(T)[:S])
    offs2 = striped8(np.stack([np.random.permutation(S)[:P] for _ in range(8)]))
    offs3 = striped8(np.stack([np.random.permutation(S)[:P] for _ in range(8)]))
    return {
        "tab_words": tab_words, "tab_scales": tab_scales,
        "offs": offs, "offs2": offs2, "offs3": offs3,
        "w1": (1.3 * n((K, H)) / np.sqrt(K) / s).astype(np.float32),
        "b1": (0.5 * n(H)).astype(np.float32),
        "gain": (np.exp(0.3 * n(H)) * np.sqrt(u[:, 0])).astype(np.float32),
        "wga": np.repeat(np.random.uniform(0.5, 2.0, (8, P)), 16, axis=0).astype(np.float32),
        "wgb": np.repeat(np.random.uniform(0.5, 2.0, (8, P)), 16, axis=0).astype(np.float32),
        "w2": (2.0 * n((H, N)) / np.sqrt(H) / u).astype(np.float32),
        "w4_words": w4_words, "w4_scales": w4_scales,
    }

def reference(tab_words, tab_scales, offs, offs2, offs3, w1, b1, gain, wga, wgb, w2, w4_words, w4_scales):
    v = unpack_weight(tab_words, tab_scales, "e4m3")[:, unstriped(offs)]
    w4 = unpack_weight(w4_words, w4_scales, "e2m1")
    a1 = (mxq(f64(w1), 0, "e4m3").T @ v) + f64(b1)[:, None]
    h = np.tanh(a1) * f64(gain)[:, None]
    xa = heads(h, f64(wga), unstriped8(offs2))
    xb = heads(h, f64(wgb), unstriped8(offs3))
    z = mxq(xa * xb, 0, "e4m3")
    y1 = mxq(f64(w2), 0, "e4m3").T @ z
    y2 = w4.T @ z
    return y1 / (1.0 + np.abs(y2))

@@ -1,0 +1,268 @@
+from contextlib import ExitStack
+
+import concourse.mybir as mybir
+
+K, T, S, H, M, N = 1024, 4096, 1024, 1024, 512, 512
+FLOPS = 2 * K * H * S + 4 * H * N * M
+
+F32 = mybir.dt.float32
+BF16 = mybir.dt.bfloat16
+I32 = mybir.dt.int32
+U32 = mybir.dt.uint32
+U16 = mybir.dt.uint16
+U8 = mybir.dt.uint8
+FP8X4 = mybir.dt.float8_e4m3fn_x4
+FP4X4 = mybir.dt.float4_e2m1fn_x4
+ACT = mybir.ActivationFunctionType
+MULT = mybir.AluOpType.mult
+
+P = 128
+PACK = 4
+PASS = P * PACK
+BANK = 512
+CHUNKS = ((0, 256), (256, 384), (384, 512))
+
+
+def tile_list_connectome_homology_scores_kernel(
+    tc, tab_words, tab_scales, offs, offs2, offs3, w1, b1, gain, wga, wgb, w2, w4_words, w4_scales, out
+):
+    nc = tc.nc
+    with ExitStack() as ctx:
+        lists = ctx.enter_context(tc.tile_pool(name="lists", bufs=1))
+        keep = ctx.enter_context(tc.tile_pool(name="keep", bufs=1))
+        ring = ctx.enter_context(tc.tile_pool(name="ring", bufs=2))
+        psum = ctx.enter_context(tc.psum_pool(name="psum", bufs=1))
+
+        def held(name, shape, dtype, tag=None):
+            return keep.tile(shape, dtype, name=name, tag=tag or name, align_bytes=64)
+
+        def bank(index, name):
+            return psum.tile([P, BANK], F32, name=name, tag="bank%d" % index)
+
+        idx = lists.tile([P, S // 16], U16, name="idx")
+        idx2 = lists.tile([P, M // 16], U16, name="idx2")
+        idx3 = lists.tile([P, M // 16], U16, name="idx3")
+        nc.sync.dma_start(idx[:], offs)
+
+        table = [held("table%d" % a, [P, T], I32, tag="big%d" % a) for a in range(2)]
+        for a in range(2):
+            nc.sync.dma_start(table[a][:], tab_words[a].rearrange("p t i -> p (t i)").bitcast(I32))
+
+        def load_rows(name, src, a, c0, c1, tag=None):
+            raw = held(name, [P, PACK, c1 - c0], F32, tag=tag)
+            nc.sync.dma_start(raw[:], src[a * PASS : (a + 1) * PASS, c0:c1].rearrange("(p j) c -> p j c", j=PACK))
+            return raw
+
+        w1_raw = {(0, 0): [load_rows("w1_raw00", w1, 0, 0, PASS)]}
+        w1_raw[0, 1] = [load_rows("w1_raw01_%d" % u, w1, 1, 256 * u, 256 * (u + 1)) for u in range(2)]
+        bias = held("bias", [P, 2, PACK], F32)
+        gains = held("gains", [P, 2, PACK], F32)
+        nc.sync.dma_start(bias[:], b1.rearrange("(b p i) -> p b i", b=2, i=PACK))
+        nc.sync.dma_start(gains[:], gain.rearrange("(b p i) -> p b i", b=2, i=PACK))
+        wa = held("wa", [P, M], F32)
+        wb = held("wb", [P, M], F32)
+        nc.sync.dma_start(wa[:], wga)
+        nc.sync.dma_start(wb[:], wgb)
+        nc.sync.dma_start(idx2[:], offs2)
+        nc.sync.dma_start(idx3[:], offs3)
+        for a in range(2):
+            w1_raw[1, a] = [load_rows("w1_raw1%d" % a, w1, a, PASS, 2 * PASS)]
+
+        table_scales = held("table_scales", [P, T], U8)
+        nc.gpsimd.memset(table_scales[:].bitcast(I32), 0)
+        for q in range(4):
+            nc.gpsimd.dma_start(
+                table_scales[32 * q : 32 * q + 8, :].bitcast(I32),
+                tab_scales[:, 4 * q : 4 * q + 4, :].bitcast(I32),
+            )
+        w4_sc = held("w4_sc", [P, 2, N], U8)
+        nc.vector.memset(w4_sc[:].rearrange("p b n -> p (b n)").bitcast(I32), 0)
+
+        v_words = [held("v_words%d" % a, [P, S], U32) for a in range(2)]
+        v_scales = held("v_scales", [P, S], U8)
+        nc.vector.tensor_copy(v_words[0][:], table[0][:].bitcast(U32).indirect(idx[:]))
+        nc.vector.tensor_copy(v_scales[:], table_scales[:].indirect(idx[:]))
+        nc.vector.tensor_copy(v_words[1][:], table[1][:].bitcast(U32).indirect(idx[:]))
+
+        w2_raw = [load_rows("w2_raw%d" % b, w2, b, 0, N, tag="big%d" % b) for b in range(2)]
+        w4_w = held("w4_w", [P, 2, 2 * N], U8)
+        nc.sync.dma_start(w4_w[:].bitcast(I32), w4_words.rearrange("b p c -> p b c").bitcast(I32))
+        for q in range(4):
+            nc.sync.dma_start(
+                w4_sc[32 * q : 32 * q + 4, :, :].bitcast(I32),
+                w4_scales[:, 4 * q : 4 * q + 4, :].rearrange("b r n -> r b n").bitcast(I32),
+            )
+
+        w1_codes, w1_scales = {}, {}
+
+        def round_w1(b, a, copy):
+            rounded = held("w1_rounded%d%d" % (b, a), [P, PACK, P, PACK], BF16, tag="w1_rounded%d" % a)
+            m0 = 0
+            for raw in w1_raw[b, a]:
+                m1 = m0 + raw.shape[2] // PACK
+                copy(
+                    rounded[:, :, m0:m1, :].rearrange("p t m j -> p m j t"),
+                    raw[:].rearrange("p j (m t) -> p m j t", t=PACK),
+                )
+                m0 = m1
+            return rounded
+
+        def quantize(codes, scales, rounded):
+            nc.vector.quantize_mx(out=codes.bitcast(FP8X4), scales=scales, in_=rounded)
+
+        def quantize_w1(b, a, rounded, cuts):
+            tag = "z_rounded0" if (b, a) == (1, 1) else None
+            w1_codes[b, a] = held("w1_codes%d%d" % (b, a), [P, PASS], U32, tag=tag)
+            w1_scales[b, a] = held("w1_scales%d%d" % (b, a), [P, PASS], U8)
+            flat = rounded[:].rearrange("p t m j -> p (t m j)")
+            for c0, c1 in cuts:
+                quantize(w1_codes[b, a][:, c0:c1], w1_scales[b, a][:, c0:c1], flat[:, PACK * c0 : PACK * c1])
+
+        h = {}
+
+        def make_h(b, i):
+            h[b, i] = held("h%d%d" % (b, i), [P, S], F32)
+            acc = [bank(2 * i + u, "h_acc%d%d%d" % (b, i, u)) for u in range(2)]
+            cols = slice(P * i, P * (i + 1))
+            for a in range(2):
+                for u in range(2):
+                    picked = slice(BANK * u, BANK * (u + 1))
+                    nc.tensor.matmul_mx(
+                        out=acc[u][:],
+                        lhsT=w1_codes[b, a][:, cols].bitcast(FP8X4),
+                        lhsT_scale=w1_scales[b, a][:, cols],
+                        rhs=v_words[a][:, picked].bitcast(FP8X4),
+                        rhs_scale=v_scales[4 * a :, picked],
+                        start=(a == 0),
+                        stop=(a == 1),
+                    )
+            for u in range(2):
+                nc.scalar.activation(
+                    h[b, i][:, BANK * u : BANK * (u + 1)], acc[u][:], ACT.Tanh, bias=bias[:, b, i : i + 1]
+                )
+
+        quantize_w1(0, 0, round_w1(0, 0, nc.scalar.copy), [(0, PASS)])
+        quantize_w1(0, 1, round_w1(0, 1, nc.vector.tensor_copy), [(0, P), (P, PASS)])
+        for i in range(PACK):
+            make_h(0, i)
+
+        wab = held("wab", [P, M], F32)
+        nc.vector.tensor_tensor(wab[:], wa[:], wb[:], MULT)
+        weight = {}
+        for b in range(2):
+            for i in range(PACK):
+                weight[b, i] = held("weight%d%d" % (b, i), [P, M], F32)
+                g = gains[:, b, i : i + 1]
+                nc.vector.tensor_scalar(weight[b, i][:], wab[:], g, g, MULT, MULT)
+
+        quantize_w1(1, 0, round_w1(1, 0, nc.scalar.copy), [(0, PASS)])
+        quantize_w1(1, 1, round_w1(1, 1, nc.vector.tensor_copy), [(0, PASS)])
+        for i in range(PACK):
+            make_h(1, i)
+
+        def pick_z(b, m0, m1, name, tags):
+            z = held(name, [P, PACK, m1 - m0], F32)
+            cols = slice(m0 // 16, m1 // 16)
+            front = held(name + "_front", [P, PACK - 1, m1 - m0], F32, tag=tags[0])
+            back = held(name + "_back", [P, m1 - m0], F32, tag=tags[1])
+            left = [front[:, i, :] for i in range(PACK - 1)] + [back[:]]
+
+            def first(i):
+                nc.vector.tensor_tensor(left[i], h[b, i][:].indirect(idx2[:, cols]), weight[b, i][:, m0:m1], MULT)
+
+            def second(i):
+                nc.vector.tensor_tensor(z[:, i, :], h[b, i][:].indirect(idx3[:, cols]), left[i], MULT)
+
+            first(0)
+            for i in range(1, PACK):
+                first(i)
+                second(i - 1)
+            second(PACK - 1)
+            return z
+
+        def interleave(name, src, copy, tag=None):
+            width = src.shape[2]
+            rounded = held(name, [P, width, PACK], BF16, tag=tag)
+            copy(
+                rounded[:].rearrange("p (c e) j -> p c j e", e=4), src[:].rearrange("p j (c e) -> p c j e", e=4)
+            )
+            return rounded
+
+        def quantize_tile(name, rounded):
+            width = rounded.shape[1]
+            codes = held(name + "_codes", [P, width], U32)
+            scales = held(name + "_scales", [P, width], U8)
+            quantize(codes[:], scales[:], rounded[:].rearrange("p c j -> p (c j)"))
+            return codes, scales
+
+        z0 = pick_z(0, 0, M, "z0", ["z0_front", "w1_rounded1"])
+        z0_q = quantize_tile("z0", interleave("z_rounded0", z0, nc.scalar.copy))
+        w2_q = [
+            quantize_tile("w2_%d" % b, interleave("w2_rounded%d" % b, w2_raw[b], nc.scalar.copy)) for b in range(2)
+        ]
+
+        y1, y2 = {}, {}
+        free = 0
+        for c, (m0, m1) in enumerate(CHUNKS):
+            per_bank = BANK // (m1 - m0)
+            count = PACK // per_bank
+            y2[c] = [bank(free + e, "y2_%d%d" % (c, e)) for e in range(count)]
+            y1[c] = [bank(free + count + e, "y1_%d%d" % (c, e)) for e in range(count)]
+            free = free + 2 * count
+
+        def products(c, b, z_codes, z_scales):
+            m0, m1 = CHUNKS[c]
+            width = m1 - m0
+            per_bank = BANK // width
+            for t in range(PACK):
+                nc.tensor.matmul_mx(
+                    out=y2[c][t // per_bank][:, width * (t % per_bank) : width * (t % per_bank + 1)],
+                    lhsT=w4_w[:, b, 2 * P * t : 2 * P * (t + 1)].bitcast(FP4X4),
+                    lhsT_scale=w4_sc[:, b, P * t : P * (t + 1)],
+                    rhs=z_codes.bitcast(FP8X4),
+                    rhs_scale=z_scales,
+                    start=(b == 0 and t % per_bank == 0),
+                    stop=(b == 1 and t % per_bank == per_bank - 1),
+                )
+            for t in range(PACK):
+                nc.tensor.matmul_mx(
+                    out=y1[c][t // per_bank][:, width * (t % per_bank) : width * (t % per_bank + 1)],
+                    lhsT=w2_q[b][0][:, P * t : P * (t + 1)].bitcast(FP8X4),
+                    lhsT_scale=w2_q[b][1][:, P * t : P * (t + 1)],
+                    rhs=z_codes.bitcast(FP8X4),
+                    rhs_scale=z_scales,
+                    start=(b == 0 and t % per_bank == 0),
+                    stop=(b == 1 and t % per_bank == per_bank - 1),
+                )
+
+        for c, (m0, m1) in enumerate(CHUNKS):
+            products(c, 0, z0_q[0][:, m0:m1], z0_q[1][:, m0:m1])
+
+        out_rows = out.rearrange("(t p) m -> p t m", p=P)
+
+        def finish(c):
+            m0, m1 = CHUNKS[c]
+            width = m1 - m0
+            per_bank = BANK // width
+            for e in range(len(y1[c])):
+                size = ring.tile([P, BANK], F32, name="size")
+                root = ring.tile([P, BANK], F32, name="root")
+                half = ring.tile([P, BANK], F32, name="half")
+                result = held("result%d%d" % (c, e), [P, BANK], F32)
+                nc.scalar.activation(size[:], y2[c][e][:], ACT.Abs)
+                nc.scalar.activation(root[:], size[:], ACT.Abs_reciprocal_sqrt, bias=1.0)
+                nc.vector.tensor_tensor(half[:], y1[c][e][:], root[:], MULT)
+                nc.vector.tensor_tensor(result[:], half[:], root[:], MULT)
+                nc.sync.dma_start(
+                    out_rows[:, per_bank * e : per_bank * (e + 1), m0:m1],
+                    result[:].rearrange("p (t m) -> p t m", m=width),
+                )
+
+        last_back, next_back = "w1_rounded1", "z1_back0"
+        for c, (m0, m1) in enumerate(CHUNKS):
+            z1 = pick_z(1, m0, m1, "z1_%d" % c, [last_back, next_back])
+            copy = nc.vector.tensor_copy if c == len(CHUNKS) - 1 else nc.scalar.copy
+            codes, scales = quantize_tile("z1_%d" % c, interleave("z1_rounded%d" % c, z1, copy))
+            last_back, next_back = next_back, "z1_rounded%d" % c
+            products(c, 1, codes[:], scales[:])
+            finish(c)

@@ -20,7 +20,7 @@ P = 128
 PACK = 4
 PASS = P * PACK
 BANK = 512
-CHUNKS = ((0, 256), (256, 384), (384, 512))
+CHUNKS = ((0, 128), (128, 256), (256, 384), (384, 512))
 
 
 def tile_list_connectome_homology_scores_kernel(
@@ -30,7 +30,7 @@ def tile_list_connectome_homology_scores_kernel(
     with ExitStack() as ctx:
         lists = ctx.enter_context(tc.tile_pool(name="lists", bufs=1))
         keep = ctx.enter_context(tc.tile_pool(name="keep", bufs=1))
-        ring = ctx.enter_context(tc.tile_pool(name="ring", bufs=2))
+        ring = ctx.enter_context(tc.tile_pool(name="ring", bufs=4))
         psum = ctx.enter_context(tc.psum_pool(name="psum", bufs=1))
 
         def held(name, shape, dtype, tag=None):
@@ -43,10 +43,30 @@ def tile_list_connectome_homology_scores_kernel(
         idx2 = lists.tile([P, M // 16], U16, name="idx2")
         idx3 = lists.tile([P, M // 16], U16, name="idx3")
         nc.sync.dma_start(idx[:], offs)
+        table_scales = held("table_scales", [P, T], U8)
+        nc.vector.memset(table_scales[:].bitcast(I32), 0)
+
+        gains = held("gains", [P, 2, 2 * PACK], F32)
+        nc.sync.dma_start(gains[:, :, :PACK], gain.rearrange("(b p i) -> p b i", b=2, i=PACK))
+        wa = held("wa", [P, M], F32)
+        wb = held("wb", [P, M], F32)
+        nc.sync.dma_start(wa[:], wga)
+        nc.sync.dma_start(wb[:], wgb)
 
         table = [held("table%d" % a, [P, T], I32, tag="big%d" % a) for a in range(2)]
-        for a in range(2):
+
+        def load_table(a):
             nc.sync.dma_start(table[a][:], tab_words[a].rearrange("p t i -> p (t i)").bitcast(I32))
+
+        def load_scale_rows(a, r):
+            nc.sync.dma_start(table_scales[4 * a + r : P : 32, :].bitcast(I32), tab_scales[a, r:16:4, :].bitcast(I32))
+
+        scale_rows = [(a, r) for r in range(4) for a in range(2)]
+        for a, r in scale_rows[:3]:
+            load_scale_rows(a, r)
+        load_table(0)
+        for a, r in scale_rows[3:]:
+            load_scale_rows(a, r)
 
         def load_rows(name, src, a, c0, c1, tag=None):
             raw = held(name, [P, PACK, c1 - c0], F32, tag=tag)
@@ -54,27 +74,15 @@ def tile_list_connectome_homology_scores_kernel(
             return raw
 
         w1_raw = {(0, 0): [load_rows("w1_raw00", w1, 0, 0, PASS)]}
+        load_table(1)
         w1_raw[0, 1] = [load_rows("w1_raw01_%d" % u, w1, 1, 256 * u, 256 * (u + 1)) for u in range(2)]
-        bias = held("bias", [P, 2, PACK], F32)
-        gains = held("gains", [P, 2, PACK], F32)
-        nc.sync.dma_start(bias[:], b1.rearrange("(b p i) -> p b i", b=2, i=PACK))
-        nc.sync.dma_start(gains[:], gain.rearrange("(b p i) -> p b i", b=2, i=PACK))
-        wa = held("wa", [P, M], F32)
-        wb = held("wb", [P, M], F32)
-        nc.sync.dma_start(wa[:], wga)
-        nc.sync.dma_start(wb[:], wgb)
+        bias = held("bias", [P, 2, 2 * PACK], F32)
+        nc.sync.dma_start(bias[:, :, :PACK], b1.rearrange("(b p i) -> p b i", b=2, i=PACK))
         nc.sync.dma_start(idx2[:], offs2)
         nc.sync.dma_start(idx3[:], offs3)
         for a in range(2):
             w1_raw[1, a] = [load_rows("w1_raw1%d" % a, w1, a, PASS, 2 * PASS)]
 
-        table_scales = held("table_scales", [P, T], U8)
-        nc.gpsimd.memset(table_scales[:].bitcast(I32), 0)
-        for q in range(4):
-            nc.gpsimd.dma_start(
-                table_scales[32 * q : 32 * q + 8, :].bitcast(I32),
-                tab_scales[:, 4 * q : 4 * q + 4, :].bitcast(I32),
-            )
         w4_sc = held("w4_sc", [P, 2, N], U8)
         nc.vector.memset(w4_sc[:].rearrange("p b n -> p (b n)").bitcast(I32), 0)
 
@@ -83,7 +91,6 @@ def tile_list_connectome_homology_scores_kernel(
         nc.vector.tensor_copy(v_words[0][:], table[0][:].bitcast(U32).indirect(idx[:]))
         nc.vector.tensor_copy(v_scales[:], table_scales[:].indirect(idx[:]))
         nc.vector.tensor_copy(v_words[1][:], table[1][:].bitcast(U32).indirect(idx[:]))
-
         w2_raw = [load_rows("w2_raw%d" % b, w2, b, 0, N, tag="big%d" % b) for b in range(2)]
         w4_w = held("w4_w", [P, 2, 2 * N], U8)
         nc.sync.dma_start(w4_w[:].bitcast(I32), w4_words.rearrange("b p c -> p b c").bitcast(I32))
@@ -95,10 +102,10 @@ def tile_list_connectome_homology_scores_kernel(
 
         w1_codes, w1_scales = {}, {}
 
-        def round_w1(b, a, copy):
+        def round_w1(b, a, *copies):
             rounded = held("w1_rounded%d%d" % (b, a), [P, PACK, P, PACK], BF16, tag="w1_rounded%d" % a)
             m0 = 0
-            for raw in w1_raw[b, a]:
+            for raw, copy in zip(w1_raw[b, a], copies):
                 m1 = m0 + raw.shape[2] // PACK
                 copy(
                     rounded[:, :, m0:m1, :].rearrange("p t m j -> p m j t"),
@@ -142,9 +149,12 @@ def tile_list_connectome_homology_scores_kernel(
                 )
 
         quantize_w1(0, 0, round_w1(0, 0, nc.scalar.copy), [(0, PASS)])
-        quantize_w1(0, 1, round_w1(0, 1, nc.vector.tensor_copy), [(0, P), (P, PASS)])
-        for i in range(PACK):
-            make_h(0, i)
+        quantize_w1(0, 1, round_w1(0, 1, nc.scalar.copy, nc.vector.tensor_copy), [(0, P), (P, PASS)])
+        make_h(0, 0)
+        make_h(0, 1)
+        w1_rounded10 = round_w1(1, 0, nc.scalar.copy)
+        make_h(0, 2)
+        make_h(0, 3)
 
         wab = held("wab", [P, M], F32)
         nc.vector.tensor_tensor(wab[:], wa[:], wb[:], MULT)
@@ -155,17 +165,17 @@ def tile_list_connectome_homology_scores_kernel(
                 g = gains[:, b, i : i + 1]
                 nc.vector.tensor_scalar(weight[b, i][:], wab[:], g, g, MULT, MULT)
 
-        quantize_w1(1, 0, round_w1(1, 0, nc.scalar.copy), [(0, PASS)])
+        quantize_w1(1, 0, w1_rounded10, [(0, PASS)])
         quantize_w1(1, 1, round_w1(1, 1, nc.vector.tensor_copy), [(0, PASS)])
         for i in range(PACK):
             make_h(1, i)
 
-        def pick_z(b, m0, m1, name, tags):
-            z = held(name, [P, PACK, m1 - m0], F32)
+        def pick_z(b, m0, m1, name, tags, z_tag=None):
+            z = held(name, [P, PACK, m1 - m0], F32, tag=z_tag)
             cols = slice(m0 // 16, m1 // 16)
-            front = held(name + "_front", [P, PACK - 1, m1 - m0], F32, tag=tags[0])
-            back = held(name + "_back", [P, m1 - m0], F32, tag=tags[1])
-            left = [front[:, i, :] for i in range(PACK - 1)] + [back[:]]
+            front = held(name + "_front", [P, 2, m1 - m0], F32, tag=tags[0])
+            back = held(name + "_back", [P, 2, m1 - m0], F32, tag=tags[1])
+            left = [front[:, 0, :], front[:, 1, :], back[:, 0, :], back[:, 1, :]]
 
             def first(i):
                 nc.vector.tensor_tensor(left[i], h[b, i][:].indirect(idx2[:, cols]), weight[b, i][:, m0:m1], MULT)
@@ -173,11 +183,11 @@ def tile_list_connectome_homology_scores_kernel(
             def second(i):
                 nc.vector.tensor_tensor(z[:, i, :], h[b, i][:].indirect(idx3[:, cols]), left[i], MULT)
 
-            first(0)
-            for i in range(1, PACK):
+            for i in (0, 2):
                 first(i)
-                second(i - 1)
-            second(PACK - 1)
+                first(i + 1)
+                second(i)
+                second(i + 1)
             return z
 
         def interleave(name, src, copy, tag=None):
@@ -195,10 +205,11 @@ def tile_list_connectome_homology_scores_kernel(
             quantize(codes[:], scales[:], rounded[:].rearrange("p c j -> p (c j)"))
             return codes, scales
 
-        z0 = pick_z(0, 0, M, "z0", ["z0_front", "w1_rounded1"])
+        z0 = pick_z(0, 0, M, "z0", ["z0_front", "w1_rounded1"], "w1_rounded0")
         z0_q = quantize_tile("z0", interleave("z_rounded0", z0, nc.scalar.copy))
         w2_q = [
-            quantize_tile("w2_%d" % b, interleave("w2_rounded%d" % b, w2_raw[b], nc.scalar.copy)) for b in range(2)
+            quantize_tile("w2_%d" % b, interleave("w2_rounded%d" % b, w2_raw[b], nc.scalar.copy, tag))
+            for b, tag in enumerate((None, "w1_rounded0"))
         ]
 
         y1, y2 = {}, {}
@@ -244,21 +255,28 @@ def tile_list_connectome_homology_scores_kernel(
             m0, m1 = CHUNKS[c]
             width = m1 - m0
             per_bank = BANK // width
-            for e in range(len(y1[c])):
-                size = ring.tile([P, BANK], F32, name="size")
-                root = ring.tile([P, BANK], F32, name="root")
-                half = ring.tile([P, BANK], F32, name="half")
-                result = held("result%d%d" % (c, e), [P, BANK], F32)
-                nc.scalar.activation(size[:], y2[c][e][:], ACT.Abs)
-                nc.scalar.activation(root[:], size[:], ACT.Abs_reciprocal_sqrt, bias=1.0)
-                nc.vector.tensor_tensor(half[:], y1[c][e][:], root[:], MULT)
-                nc.vector.tensor_tensor(result[:], half[:], root[:], MULT)
+            size = ring.tile([P, BANK], F32, name="size")
+            root = ring.tile([P, BANK], F32, name="root")
+            half = ring.tile([P, BANK], F32, name="half")
+            result = ring.tile([P, BANK], F32, name="result")
+            last = c == len(CHUNKS) - 1
+            pieces = 2 if last else 1
+            for e in range(pieces):
+                t0, t1 = PACK // pieces * e, PACK // pieces * (e + 1)
+                cols = slice(width * t0, width * t1)
+                nc.scalar.activation(size[:, cols], y2[c][0][:, cols], ACT.Abs)
+                nc.scalar.activation(root[:, cols], size[:, cols], ACT.Abs_reciprocal_sqrt, bias=1.0)
+                if last:
+                    nc.vector.tensor_tensor(half[:, cols], y1[c][0][:, cols], root[:, cols], MULT)
+                    nc.vector.tensor_tensor(result[:, cols], half[:, cols], root[:, cols], MULT)
+                else:
+                    nc.scalar.activation(half[:, cols], root[:, cols], ACT.Square)
+                    nc.vector.tensor_tensor(result[:, cols], y1[c][0][:, cols], half[:, cols], MULT)
                 nc.sync.dma_start(
-                    out_rows[:, per_bank * e : per_bank * (e + 1), m0:m1],
-                    result[:].rearrange("p (t m) -> p t m", m=width),
+                    out_rows[:, t0:t1, m0:m1], result[:, cols].rearrange("p (t m) -> p t m", m=width)
                 )
 
-        last_back, next_back = "w1_rounded1", "z1_back0"
+        last_back, next_back = "w1_rounded1", "z_rounded0"
         for c, (m0, m1) in enumerate(CHUNKS):
             z1 = pick_z(1, m0, m1, "z1_%d" % c, [last_back, next_back])
             copy = nc.vector.tensor_copy if c == len(CHUNKS) - 1 else nc.scalar.copy

@@ -20,7 +20,7 @@ P = 128
 PACK = 4
 PASS = P * PACK
 BANK = 512
-CHUNKS = ((0, 128), (128, 256), (256, 384), (384, 512))
+CHUNKS = ((0, 256), (256, 384), (384, 512))
 
 
 def tile_list_connectome_homology_scores_kernel(
@@ -30,7 +30,7 @@ def tile_list_connectome_homology_scores_kernel(
     with ExitStack() as ctx:
         lists = ctx.enter_context(tc.tile_pool(name="lists", bufs=1))
         keep = ctx.enter_context(tc.tile_pool(name="keep", bufs=1))
-        ring = ctx.enter_context(tc.tile_pool(name="ring", bufs=4))
+        ring = ctx.enter_context(tc.tile_pool(name="ring", bufs=5))
         psum = ctx.enter_context(tc.psum_pool(name="psum", bufs=1))
 
         def held(name, shape, dtype, tag=None):
@@ -47,7 +47,9 @@ def tile_list_connectome_homology_scores_kernel(
         nc.vector.memset(table_scales[:].bitcast(I32), 0)
 
         gains = held("gains", [P, 2, 2 * PACK], F32)
-        nc.sync.dma_start(gains[:, :, :PACK], gain.rearrange("(b p i) -> p b i", b=2, i=PACK))
+        bias = held("bias", [P, 2, 2 * PACK], F32)
+        nc.scalar.dma_start(gains[:, :, :PACK], gain.rearrange("(b p i) -> p b i", b=2, i=PACK))
+        nc.scalar.dma_start(bias[:, :, :PACK], b1.rearrange("(b p i) -> p b i", b=2, i=PACK))
         wa = held("wa", [P, M], F32)
         wb = held("wb", [P, M], F32)
         nc.sync.dma_start(wa[:], wga)
@@ -62,10 +64,10 @@ def tile_list_connectome_homology_scores_kernel(
             nc.sync.dma_start(table_scales[4 * a + r : P : 32, :].bitcast(I32), tab_scales[a, r:16:4, :].bitcast(I32))
 
         scale_rows = [(a, r) for r in range(4) for a in range(2)]
-        for a, r in scale_rows[:3]:
+        for a, r in scale_rows[:2]:
             load_scale_rows(a, r)
         load_table(0)
-        for a, r in scale_rows[3:]:
+        for a, r in scale_rows[2:]:
             load_scale_rows(a, r)
 
         def load_rows(name, src, a, c0, c1, tag=None):
@@ -76,8 +78,6 @@ def tile_list_connectome_homology_scores_kernel(
         w1_raw = {(0, 0): [load_rows("w1_raw00", w1, 0, 0, PASS)]}
         load_table(1)
         w1_raw[0, 1] = [load_rows("w1_raw01_%d" % u, w1, 1, 256 * u, 256 * (u + 1)) for u in range(2)]
-        bias = held("bias", [P, 2, 2 * PACK], F32)
-        nc.sync.dma_start(bias[:, :, :PACK], b1.rearrange("(b p i) -> p b i", b=2, i=PACK))
         nc.sync.dma_start(idx2[:], offs2)
         nc.sync.dma_start(idx3[:], offs3)
         for a in range(2):
@@ -221,33 +221,33 @@ def tile_list_connectome_homology_scores_kernel(
             y1[c] = [bank(free + count + e, "y1_%d%d" % (c, e)) for e in range(count)]
             free = free + 2 * count
 
-        def products(c, b, z_codes, z_scales):
-            m0, m1 = CHUNKS[c]
-            width = m1 - m0
-            per_bank = BANK // width
-            for t in range(PACK):
-                nc.tensor.matmul_mx(
-                    out=y2[c][t // per_bank][:, width * (t % per_bank) : width * (t % per_bank + 1)],
-                    lhsT=w4_w[:, b, 2 * P * t : 2 * P * (t + 1)].bitcast(FP4X4),
-                    lhsT_scale=w4_sc[:, b, P * t : P * (t + 1)],
-                    rhs=z_codes.bitcast(FP8X4),
-                    rhs_scale=z_scales,
-                    start=(b == 0 and t % per_bank == 0),
-                    stop=(b == 1 and t % per_bank == per_bank - 1),
-                )
-            for t in range(PACK):
-                nc.tensor.matmul_mx(
-                    out=y1[c][t // per_bank][:, width * (t % per_bank) : width * (t % per_bank + 1)],
-                    lhsT=w2_q[b][0][:, P * t : P * (t + 1)].bitcast(FP8X4),
-                    lhsT_scale=w2_q[b][1][:, P * t : P * (t + 1)],
-                    rhs=z_codes.bitcast(FP8X4),
-                    rhs_scale=z_scales,
-                    start=(b == 0 and t % per_bank == 0),
-                    stop=(b == 1 and t % per_bank == per_bank - 1),
-                )
+        def level(c, b, t):
+            return y2[c], w4_w[:, b, 2 * P * t : 2 * P * (t + 1)].bitcast(FP4X4), w4_sc[:, b, P * t : P * (t + 1)]
 
-        for c, (m0, m1) in enumerate(CHUNKS):
-            products(c, 0, z0_q[0][:, m0:m1], z0_q[1][:, m0:m1])
+        def agreement(c, b, t):
+            cols = slice(P * t, P * (t + 1))
+            return y1[c], w2_q[b][0][:, cols].bitcast(FP8X4), w2_q[b][1][:, cols]
+
+        def products(c, b, z_codes, z_scales, kinds):
+            width = CHUNKS[c][1] - CHUNKS[c][0]
+            per_bank = BANK // width
+            for kind in kinds:
+                for t in range(PACK):
+                    banks, codes, scales = kind(c, b, t)
+                    place = t % per_bank
+                    nc.tensor.matmul_mx(
+                        out=banks[t // per_bank][:, width * place : width * (place + 1)],
+                        lhsT=codes,
+                        lhsT_scale=scales,
+                        rhs=z_codes.bitcast(FP8X4),
+                        rhs_scale=z_scales,
+                        start=(b == 0 and place == 0),
+                        stop=(b == 1 and place == per_bank - 1),
+                    )
+
+        for kind in (level, agreement):
+            for c, (m0, m1) in enumerate(CHUNKS):
+                products(c, 0, z0_q[0][:, m0:m1], z0_q[1][:, m0:m1], (kind,))
 
         out_rows = out.rearrange("(t p) m -> p t m", p=P)
 
@@ -255,32 +255,35 @@ def tile_list_connectome_homology_scores_kernel(
             m0, m1 = CHUNKS[c]
             width = m1 - m0
             per_bank = BANK // width
-            size = ring.tile([P, BANK], F32, name="size")
-            root = ring.tile([P, BANK], F32, name="root")
-            half = ring.tile([P, BANK], F32, name="half")
-            result = ring.tile([P, BANK], F32, name="result")
             last = c == len(CHUNKS) - 1
-            pieces = 2 if last else 1
+            pieces = 2 if last else len(y1[c])
             for e in range(pieces):
                 t0, t1 = PACK // pieces * e, PACK // pieces * (e + 1)
-                cols = slice(width * t0, width * t1)
-                nc.scalar.activation(size[:, cols], y2[c][0][:, cols], ACT.Abs)
-                nc.scalar.activation(root[:, cols], size[:, cols], ACT.Abs_reciprocal_sqrt, bias=1.0)
-                if last:
-                    nc.vector.tensor_tensor(half[:, cols], y1[c][0][:, cols], root[:, cols], MULT)
-                    nc.vector.tensor_tensor(result[:, cols], half[:, cols], root[:, cols], MULT)
+                cols = slice(width * (t0 % per_bank), width * (t0 % per_bank + t1 - t0))
+                size = ring.tile([P, width * (t1 - t0)], F32, name="size")
+                root = ring.tile([P, width * (t1 - t0)], F32, name="root")
+                half = ring.tile([P, width * (t1 - t0)], F32, name="half")
+                result = ring.tile([P, width * (t1 - t0)], F32, name="result")
+                nc.scalar.activation(size[:], y2[c][t0 // per_bank][:, cols], ACT.Abs)
+                nc.scalar.activation(root[:], size[:], ACT.Abs_reciprocal_sqrt, bias=1.0)
+                if (c, e) in ((1, 0), (2, 0), (2, 1)):
+                    nc.vector.tensor_tensor(half[:], y1[c][t0 // per_bank][:, cols], root[:], MULT)
+                    nc.vector.tensor_tensor(result[:], half[:], root[:], MULT)
                 else:
-                    nc.scalar.activation(half[:, cols], root[:, cols], ACT.Square)
-                    nc.vector.tensor_tensor(result[:, cols], y1[c][0][:, cols], half[:, cols], MULT)
-                nc.sync.dma_start(
-                    out_rows[:, t0:t1, m0:m1], result[:, cols].rearrange("p (t m) -> p t m", m=width)
-                )
+                    nc.scalar.activation(half[:], root[:], ACT.Square)
+                    nc.vector.tensor_tensor(result[:], y1[c][t0 // per_bank][:, cols], half[:], MULT)
+                nc.sync.dma_start(out_rows[:, t0:t1, m0:m1], result[:].rearrange("p (t m) -> p t m", m=width))
 
-        last_back, next_back = "w1_rounded1", "z_rounded0"
+        tags = [
+            ("w1_rounded1", "z_rounded0"),
+            ("z_rounded0", "z1_rounded0"),
+            ("z1_rounded0", "z1_rounded1"),
+        ]
         for c, (m0, m1) in enumerate(CHUNKS):
-            z1 = pick_z(1, m0, m1, "z1_%d" % c, [last_back, next_back])
+            z1 = pick_z(1, m0, m1, "z1_%d" % c, tags[c])
             copy = nc.vector.tensor_copy if c == len(CHUNKS) - 1 else nc.scalar.copy
             codes, scales = quantize_tile("z1_%d" % c, interleave("z1_rounded%d" % c, z1, copy))
-            last_back, next_back = next_back, "z1_rounded%d" % c
-            products(c, 1, codes[:], scales[:])
-            finish(c)
+            products(c, 1, codes[:], scales[:], (level, agreement))
+            if c > 0:
+                finish(c - 1)
+        finish(len(CHUNKS) - 1)

@@ -1,6 +1,7 @@
 from contextlib import ExitStack
 
 import concourse.mybir as mybir
+from concourse.masks import make_identity
 
 K, T, S, H, M, N = 1024, 4096, 1024, 1024, 512, 512
 FLOPS = 2 * K * H * S + 4 * H * N * M
@@ -20,7 +21,9 @@ P = 128
 PACK = 4
 PASS = P * PACK
 BANK = 512
+GROUPS = 8
 CHUNKS = ((0, 256), (256, 384), (384, 512))
+LAST = len(CHUNKS) - 1
 
 
 def tile_list_connectome_homology_scores_kernel(
@@ -30,7 +33,7 @@ def tile_list_connectome_homology_scores_kernel(
     with ExitStack() as ctx:
         lists = ctx.enter_context(tc.tile_pool(name="lists", bufs=1))
         keep = ctx.enter_context(tc.tile_pool(name="keep", bufs=1))
-        ring = ctx.enter_context(tc.tile_pool(name="ring", bufs=5))
+        ring = ctx.enter_context(tc.tile_pool(name="ring", bufs=3))
         psum = ctx.enter_context(tc.psum_pool(name="psum", bufs=1))
 
         def held(name, shape, dtype, tag=None):
@@ -48,13 +51,19 @@ def tile_list_connectome_homology_scores_kernel(
 
         gains = held("gains", [P, 2, 2 * PACK], F32)
         bias = held("bias", [P, 2, 2 * PACK], F32)
+        wa = held("wa", [GROUPS, M], F32)
+        wb = held("wb", [GROUPS, M], F32)
         nc.scalar.dma_start(gains[:, :, :PACK], gain.rearrange("(b p i) -> p b i", b=2, i=PACK))
         nc.scalar.dma_start(bias[:, :, :PACK], b1.rearrange("(b p i) -> p b i", b=2, i=PACK))
-        wa = held("wa", [P, M], F32)
-        wb = held("wb", [P, M], F32)
-        nc.sync.dma_start(wa[:], wga)
-        nc.sync.dma_start(wb[:], wgb)
+        nc.sync.dma_start(wa[:], wga[0:P:16, :])
+        nc.sync.dma_start(wb[:], wgb[0:P:16, :])
 
+        def load_rows(name, src, a, c0, c1, tag=None):
+            raw = held(name, [P, PACK, c1 - c0], F32, tag=tag)
+            nc.sync.dma_start(raw[:], src[a * PASS : (a + 1) * PASS, c0:c1].rearrange("(p j) c -> p j c", j=PACK))
+            return raw
+
+        w1_raw = {(0, 0): [load_rows("w1_raw00", w1, 0, 0, PASS)]}
         table = [held("table%d" % a, [P, T], I32, tag="big%d" % a) for a in range(2)]
 
         def load_table(a):
@@ -69,13 +78,6 @@ def tile_list_connectome_homology_scores_kernel(
         load_table(0)
         for a, r in scale_rows[2:]:
             load_scale_rows(a, r)
-
-        def load_rows(name, src, a, c0, c1, tag=None):
-            raw = held(name, [P, PACK, c1 - c0], F32, tag=tag)
-            nc.sync.dma_start(raw[:], src[a * PASS : (a + 1) * PASS, c0:c1].rearrange("(p j) c -> p j c", j=PACK))
-            return raw
-
-        w1_raw = {(0, 0): [load_rows("w1_raw00", w1, 0, 0, PASS)]}
         load_table(1)
         w1_raw[0, 1] = [load_rows("w1_raw01_%d" % u, w1, 1, 256 * u, 256 * (u + 1)) for u in range(2)]
         nc.sync.dma_start(idx2[:], offs2)
@@ -85,6 +87,32 @@ def tile_list_connectome_homology_scores_kernel(
 
         w4_sc = held("w4_sc", [P, 2, N], U8)
         nc.vector.memset(w4_sc[:].rearrange("p b n -> p (b n)").bitcast(I32), 0)
+
+        identity = held("identity", [P, P], F32)
+        make_identity(nc, identity[:])
+        by_group = held("by_group", [P, M], F32)
+        nc.gpsimd.memset(by_group[:], 0.0)
+        nc.vector.tensor_tensor(by_group[:GROUPS, :], wa[:], wb[:], MULT)
+        turned = bank(6, "turned")
+        for j in range(M // P):
+            nc.tensor.transpose(turned[:, P * j : P * (j + 1)], by_group[:, P * j : P * (j + 1)], identity[:])
+        spread = held("spread", [P, M // P, GROUPS, 16], F32)
+        nc.vector.tensor_copy(
+            spread[:],
+            turned[:].rearrange("m (j g s) -> m j g s", g=P, s=1)[:, :, :GROUPS, :].to_broadcast([P, M // P, GROUPS, 16]),
+        )
+        back_turned = bank(7, "back_turned")
+        for j in range(M // P):
+            nc.tensor.transpose(
+                back_turned[:, P * j : P * (j + 1)], spread[:, j, :, :].rearrange("m g s -> m (g s)"), identity[:]
+            )
+        gains2 = held("gains2", [P, 2, PACK], F32)
+        nc.scalar.activation(gains2[:], gains[:, :, :PACK], ACT.Square)
+        weight = {}
+        for b in range(2):
+            for i in range(PACK):
+                weight[b, i] = held("weight%d%d" % (b, i), [P, M], F32)
+                nc.scalar.activation(weight[b, i][:], back_turned[:], ACT.Copy, scale=gains2[:, b, i : i + 1])
 
         v_words = [held("v_words%d" % a, [P, S], U32) for a in range(2)]
         v_scales = held("v_scales", [P, S], U8)
@@ -155,15 +183,6 @@ def tile_list_connectome_homology_scores_kernel(
         w1_rounded10 = round_w1(1, 0, nc.scalar.copy)
         make_h(0, 2)
         make_h(0, 3)
-
-        wab = held("wab", [P, M], F32)
-        nc.vector.tensor_tensor(wab[:], wa[:], wb[:], MULT)
-        weight = {}
-        for b in range(2):
-            for i in range(PACK):
-                weight[b, i] = held("weight%d%d" % (b, i), [P, M], F32)
-                g = gains[:, b, i : i + 1]
-                nc.vector.tensor_scalar(weight[b, i][:], wab[:], g, g, MULT, MULT)
 
         quantize_w1(1, 0, w1_rounded10, [(0, PASS)])
         quantize_w1(1, 1, round_w1(1, 1, nc.vector.tensor_copy), [(0, PASS)])
@@ -251,29 +270,36 @@ def tile_list_connectome_homology_scores_kernel(
 
         out_rows = out.rearrange("(t p) m -> p t m", p=P)
 
-        def finish(c):
-            m0, m1 = CHUNKS[c]
-            width = m1 - m0
+        def pieces(c):
+            width = CHUNKS[c][1] - CHUNKS[c][0]
             per_bank = BANK // width
-            last = c == len(CHUNKS) - 1
-            pieces = 2 if last else len(y1[c])
-            for e in range(pieces):
-                t0, t1 = PACK // pieces * e, PACK // pieces * (e + 1)
-                cols = slice(width * (t0 % per_bank), width * (t0 % per_bank + t1 - t0))
-                size = ring.tile([P, width * (t1 - t0)], F32, name="size")
-                root = ring.tile([P, width * (t1 - t0)], F32, name="root")
-                half = ring.tile([P, width * (t1 - t0)], F32, name="half")
-                result = ring.tile([P, width * (t1 - t0)], F32, name="result")
-                nc.scalar.activation(size[:], y2[c][t0 // per_bank][:, cols], ACT.Abs)
-                nc.scalar.activation(root[:], size[:], ACT.Abs_reciprocal_sqrt, bias=1.0)
-                if (c, e) in ((1, 0), (2, 0), (2, 1)):
-                    nc.vector.tensor_tensor(half[:], y1[c][t0 // per_bank][:, cols], root[:], MULT)
-                    nc.vector.tensor_tensor(result[:], half[:], root[:], MULT)
-                else:
-                    nc.scalar.activation(half[:], root[:], ACT.Square)
-                    nc.vector.tensor_tensor(result[:], y1[c][t0 // per_bank][:, cols], half[:], MULT)
-                nc.sync.dma_start(out_rows[:, t0:t1, m0:m1], result[:].rearrange("p (t m) -> p t m", m=width))
+            tiles = 2 if c == LAST else per_bank
+            return [
+                (t // per_bank, slice(width * (t % per_bank), width * (t % per_bank + tiles)), t, t + tiles)
+                for t in range(0, PACK, tiles)
+            ]
 
+        def inverse_root(c, e, cols, tag=None):
+            size = held("size%d_%d" % (c, e * BANK + cols.start), [P, cols.stop - cols.start], F32, tag=tag)
+            root = ring.tile([P, cols.stop - cols.start], F32, name="root")
+            nc.scalar.activation(size[:], y2[c][e][:, cols], ACT.Abs)
+            nc.scalar.activation(root[:], size[:], ACT.Abs_reciprocal_sqrt, bias=1.0)
+            return root
+
+        def inverses(c, roots):
+            done = []
+            for e, cols, t0, t1 in pieces(c):
+                root = roots[e] if e < len(roots) else inverse_root(c, e, cols)
+                inverse = ring.tile([P, cols.stop - cols.start], F32, name="inverse")
+                nc.scalar.activation(inverse[:], root[:], ACT.Square)
+                done.append(inverse)
+            return done
+
+        def store(c, t0, t1, result):
+            m0, m1 = CHUNKS[c]
+            nc.sync.dma_start(out_rows[:, t0:t1, m0:m1], result.rearrange("p (t m) -> p t m", m=m1 - m0))
+
+        inverse_of = []
         tags = [
             ("w1_rounded1", "z_rounded0"),
             ("z_rounded0", "z1_rounded0"),
@@ -281,9 +307,29 @@ def tile_list_connectome_homology_scores_kernel(
         ]
         for c, (m0, m1) in enumerate(CHUNKS):
             z1 = pick_z(1, m0, m1, "z1_%d" % c, tags[c])
-            copy = nc.vector.tensor_copy if c == len(CHUNKS) - 1 else nc.scalar.copy
-            codes, scales = quantize_tile("z1_%d" % c, interleave("z1_rounded%d" % c, z1, copy))
+            copy = nc.vector.tensor_copy if c == LAST else nc.scalar.copy
+            rounded = interleave("z1_rounded%d" % c, z1, copy)
+            if c == 0:
+                unread = held("unread", [P, 1], F32)
+                nc.scalar.activation(unread[:], z1[:, PACK - 1, 0:1], ACT.Abs_reciprocal_sqrt, bias=1.0, scale=0.0)
+            codes, scales = quantize_tile("z1_%d" % c, rounded)
             products(c, 1, codes[:], scales[:], (level, agreement))
-            if c > 0:
-                finish(c - 1)
-        finish(len(CHUNKS) - 1)
+            if c == 0:
+                early = [inverse_root(0, 0, pieces(0)[0][1], "z1_rounded1")]
+            else:
+                inverse_of.append(inverses(c - 1, early if c == 1 else []))
+
+        for c in range(LAST):
+            m0, m1 = CHUNKS[c]
+            result = held("result%d" % c, [P, PACK * (m1 - m0)], F32, tag="z1_rounded%d" % LAST if c == 0 else None)
+            for (e, cols, t0, t1), inverse in zip(pieces(c), inverse_of[c]):
+                part = result[:, (m1 - m0) * t0 : (m1 - m0) * t1]
+                nc.vector.tensor_tensor(part, y1[c][e][:, cols], inverse[:], MULT)
+                store(c, t0, t1, part)
+        for e, cols, t0, t1 in pieces(LAST):
+            root = inverse_root(LAST, e, cols)
+            once = ring.tile([P, cols.stop - cols.start], F32, name="once")
+            twice = ring.tile([P, cols.stop - cols.start], F32, name="twice")
+            nc.vector.tensor_tensor(once[:], y1[LAST][e][:, cols], root[:], MULT)
+            nc.vector.tensor_tensor(twice[:], once[:], root[:], MULT)
+            store(LAST, t0, t1, twice[:])

from contextlib import ExitStack

import concourse.mybir as mybir
from concourse.masks import make_identity

K, T, S, H, M, N = 1024, 4096, 1024, 1024, 512, 512
FLOPS = 2 * K * H * S + 4 * H * N * M

F32 = mybir.dt.float32
BF16 = mybir.dt.bfloat16
I32 = mybir.dt.int32
U32 = mybir.dt.uint32
U16 = mybir.dt.uint16
U8 = mybir.dt.uint8
FP8X4 = mybir.dt.float8_e4m3fn_x4
FP4X4 = mybir.dt.float4_e2m1fn_x4
ACT = mybir.ActivationFunctionType
MULT = mybir.AluOpType.mult

P = 128
PACK = 4
PASS = P * PACK
BANK = 512
GROUPS = 8
CHUNKS = ((0, 256), (256, 384), (384, 512))
LAST = len(CHUNKS) - 1


def tile_list_connectome_homology_scores_kernel(
    tc, tab_words, tab_scales, offs, offs2, offs3, w1, b1, gain, wga, wgb, w2, w4_words, w4_scales, out
):
    nc = tc.nc
    with ExitStack() as ctx:
        lists = ctx.enter_context(tc.tile_pool(name="lists", bufs=1))
        keep = ctx.enter_context(tc.tile_pool(name="keep", bufs=1))
        ring = ctx.enter_context(tc.tile_pool(name="ring", bufs=3))
        psum = ctx.enter_context(tc.psum_pool(name="psum", bufs=1))

        def held(name, shape, dtype, tag=None):
            return keep.tile(shape, dtype, name=name, tag=tag or name, align_bytes=64)

        def bank(index, name):
            return psum.tile([P, BANK], F32, name=name, tag="bank%d" % index)

        idx = lists.tile([P, S // 16], U16, name="idx")
        idx2 = lists.tile([P, M // 16], U16, name="idx2")
        idx3 = lists.tile([P, M // 16], U16, name="idx3")
        nc.sync.dma_start(idx[:], offs)
        table_scales = held("table_scales", [P, T], U8)
        nc.vector.memset(table_scales[:].bitcast(I32), 0)

        gains = held("gains", [P, 2, 2 * PACK], F32)
        bias = held("bias", [P, 2, 2 * PACK], F32)
        wa = held("wa", [GROUPS, M], F32)
        wb = held("wb", [GROUPS, M], F32)
        nc.scalar.dma_start(gains[:, :, :PACK], gain.rearrange("(b p i) -> p b i", b=2, i=PACK))
        nc.scalar.dma_start(bias[:, :, :PACK], b1.rearrange("(b p i) -> p b i", b=2, i=PACK))
        nc.sync.dma_start(wa[:], wga[0:P:16, :])
        nc.sync.dma_start(wb[:], wgb[0:P:16, :])

        def load_rows(name, src, a, c0, c1, tag=None):
            raw = held(name, [P, PACK, c1 - c0], F32, tag=tag)
            nc.sync.dma_start(raw[:], src[a * PASS : (a + 1) * PASS, c0:c1].rearrange("(p j) c -> p j c", j=PACK))
            return raw

        w1_raw = {(0, 0): [load_rows("w1_raw00", w1, 0, 0, PASS)]}
        table = [held("table%d" % a, [P, T], I32, tag="big%d" % a) for a in range(2)]

        def load_table(a):
            nc.sync.dma_start(table[a][:], tab_words[a].rearrange("p t i -> p (t i)").bitcast(I32))

        def load_scale_rows(a, r):
            nc.sync.dma_start(table_scales[4 * a + r : P : 32, :].bitcast(I32), tab_scales[a, r:16:4, :].bitcast(I32))

        scale_rows = [(a, r) for r in range(4) for a in range(2)]
        for a, r in scale_rows[:2]:
            load_scale_rows(a, r)
        load_table(0)
        for a, r in scale_rows[2:]:
            load_scale_rows(a, r)
        load_table(1)
        w1_raw[0, 1] = [load_rows("w1_raw01_%d" % u, w1, 1, 256 * u, 256 * (u + 1)) for u in range(2)]
        nc.sync.dma_start(idx2[:], offs2)
        nc.sync.dma_start(idx3[:], offs3)
        for a in range(2):
            w1_raw[1, a] = [load_rows("w1_raw1%d" % a, w1, a, PASS, 2 * PASS)]

        w4_sc = held("w4_sc", [P, 2, N], U8)
        nc.vector.memset(w4_sc[:].rearrange("p b n -> p (b n)").bitcast(I32), 0)

        identity = held("identity", [P, P], F32)
        make_identity(nc, identity[:])
        by_group = held("by_group", [P, M], F32)
        nc.gpsimd.memset(by_group[:], 0.0)
        nc.vector.tensor_tensor(by_group[:GROUPS, :], wa[:], wb[:], MULT)
        turned = bank(6, "turned")
        for j in range(M // P):
            nc.tensor.transpose(turned[:, P * j : P * (j + 1)], by_group[:, P * j : P * (j + 1)], identity[:])
        spread = held("spread", [P, M // P, GROUPS, 16], F32)
        nc.vector.tensor_copy(
            spread[:],
            turned[:].rearrange("m (j g s) -> m j g s", g=P, s=1)[:, :, :GROUPS, :].to_broadcast([P, M // P, GROUPS, 16]),
        )
        back_turned = bank(7, "back_turned")
        for j in range(M // P):
            nc.tensor.transpose(
                back_turned[:, P * j : P * (j + 1)], spread[:, j, :, :].rearrange("m g s -> m (g s)"), identity[:]
            )
        gains2 = held("gains2", [P, 2, PACK], F32)
        nc.scalar.activation(gains2[:], gains[:, :, :PACK], ACT.Square)
        weight = {}
        for b in range(2):
            for i in range(PACK):
                weight[b, i] = held("weight%d%d" % (b, i), [P, M], F32)
                nc.scalar.activation(weight[b, i][:], back_turned[:], ACT.Copy, scale=gains2[:, b, i : i + 1])

        v_words = [held("v_words%d" % a, [P, S], U32) for a in range(2)]
        v_scales = held("v_scales", [P, S], U8)
        nc.vector.tensor_copy(v_words[0][:], table[0][:].bitcast(U32).indirect(idx[:]))
        nc.vector.tensor_copy(v_scales[:], table_scales[:].indirect(idx[:]))
        nc.vector.tensor_copy(v_words[1][:], table[1][:].bitcast(U32).indirect(idx[:]))
        w2_raw = [load_rows("w2_raw%d" % b, w2, b, 0, N, tag="big%d" % b) for b in range(2)]
        w4_w = held("w4_w", [P, 2, 2 * N], U8)
        nc.sync.dma_start(w4_w[:].bitcast(I32), w4_words.rearrange("b p c -> p b c").bitcast(I32))
        for q in range(4):
            nc.sync.dma_start(
                w4_sc[32 * q : 32 * q + 4, :, :].bitcast(I32),
                w4_scales[:, 4 * q : 4 * q + 4, :].rearrange("b r n -> r b n").bitcast(I32),
            )

        w1_codes, w1_scales = {}, {}

        def round_w1(b, a, *copies):
            rounded = held("w1_rounded%d%d" % (b, a), [P, PACK, P, PACK], BF16, tag="w1_rounded%d" % a)
            m0 = 0
            for raw, copy in zip(w1_raw[b, a], copies):
                m1 = m0 + raw.shape[2] // PACK
                copy(
                    rounded[:, :, m0:m1, :].rearrange("p t m j -> p m j t"),
                    raw[:].rearrange("p j (m t) -> p m j t", t=PACK),
                )
                m0 = m1
            return rounded

        def quantize(codes, scales, rounded):
            nc.vector.quantize_mx(out=codes.bitcast(FP8X4), scales=scales, in_=rounded)

        def quantize_w1(b, a, rounded, cuts):
            tag = "z_rounded0" if (b, a) == (1, 1) else None
            w1_codes[b, a] = held("w1_codes%d%d" % (b, a), [P, PASS], U32, tag=tag)
            w1_scales[b, a] = held("w1_scales%d%d" % (b, a), [P, PASS], U8)
            flat = rounded[:].rearrange("p t m j -> p (t m j)")
            for c0, c1 in cuts:
                quantize(w1_codes[b, a][:, c0:c1], w1_scales[b, a][:, c0:c1], flat[:, PACK * c0 : PACK * c1])

        h = {}

        def make_h(b, i):
            h[b, i] = held("h%d%d" % (b, i), [P, S], F32)
            acc = [bank(2 * i + u, "h_acc%d%d%d" % (b, i, u)) for u in range(2)]
            cols = slice(P * i, P * (i + 1))
            for a in range(2):
                for u in range(2):
                    picked = slice(BANK * u, BANK * (u + 1))
                    nc.tensor.matmul_mx(
                        out=acc[u][:],
                        lhsT=w1_codes[b, a][:, cols].bitcast(FP8X4),
                        lhsT_scale=w1_scales[b, a][:, cols],
                        rhs=v_words[a][:, picked].bitcast(FP8X4),
                        rhs_scale=v_scales[4 * a :, picked],
                        start=(a == 0),
                        stop=(a == 1),
                    )
            for u in range(2):
                nc.scalar.activation(
                    h[b, i][:, BANK * u : BANK * (u + 1)], acc[u][:], ACT.Tanh, bias=bias[:, b, i : i + 1]
                )

        quantize_w1(0, 0, round_w1(0, 0, nc.scalar.copy), [(0, PASS)])
        quantize_w1(0, 1, round_w1(0, 1, nc.scalar.copy, nc.vector.tensor_copy), [(0, P), (P, PASS)])
        make_h(0, 0)
        make_h(0, 1)
        w1_rounded10 = round_w1(1, 0, nc.scalar.copy)
        make_h(0, 2)
        make_h(0, 3)

        quantize_w1(1, 0, w1_rounded10, [(0, PASS)])
        quantize_w1(1, 1, round_w1(1, 1, nc.vector.tensor_copy), [(0, PASS)])
        for i in range(PACK):
            make_h(1, i)

        def pick_z(b, m0, m1, name, tags, z_tag=None):
            z = held(name, [P, PACK, m1 - m0], F32, tag=z_tag)
            cols = slice(m0 // 16, m1 // 16)
            front = held(name + "_front", [P, 2, m1 - m0], F32, tag=tags[0])
            back = held(name + "_back", [P, 2, m1 - m0], F32, tag=tags[1])
            left = [front[:, 0, :], front[:, 1, :], back[:, 0, :], back[:, 1, :]]

            def first(i):
                nc.vector.tensor_tensor(left[i], h[b, i][:].indirect(idx2[:, cols]), weight[b, i][:, m0:m1], MULT)

            def second(i):
                nc.vector.tensor_tensor(z[:, i, :], h[b, i][:].indirect(idx3[:, cols]), left[i], MULT)

            for i in (0, 2):
                first(i)
                first(i + 1)
                second(i)
                second(i + 1)
            return z

        def interleave(name, src, copy, tag=None):
            width = src.shape[2]
            rounded = held(name, [P, width, PACK], BF16, tag=tag)
            copy(
                rounded[:].rearrange("p (c e) j -> p c j e", e=4), src[:].rearrange("p j (c e) -> p c j e", e=4)
            )
            return rounded

        def quantize_tile(name, rounded):
            width = rounded.shape[1]
            codes = held(name + "_codes", [P, width], U32)
            scales = held(name + "_scales", [P, width], U8)
            quantize(codes[:], scales[:], rounded[:].rearrange("p c j -> p (c j)"))
            return codes, scales

        z0 = pick_z(0, 0, M, "z0", ["z0_front", "w1_rounded1"], "w1_rounded0")
        z0_q = quantize_tile("z0", interleave("z_rounded0", z0, nc.scalar.copy))
        w2_q = [
            quantize_tile("w2_%d" % b, interleave("w2_rounded%d" % b, w2_raw[b], nc.scalar.copy, tag))
            for b, tag in enumerate((None, "w1_rounded0"))
        ]

        y1, y2 = {}, {}
        free = 0
        for c, (m0, m1) in enumerate(CHUNKS):
            per_bank = BANK // (m1 - m0)
            count = PACK // per_bank
            y2[c] = [bank(free + e, "y2_%d%d" % (c, e)) for e in range(count)]
            y1[c] = [bank(free + count + e, "y1_%d%d" % (c, e)) for e in range(count)]
            free = free + 2 * count

        def level(c, b, t):
            return y2[c], w4_w[:, b, 2 * P * t : 2 * P * (t + 1)].bitcast(FP4X4), w4_sc[:, b, P * t : P * (t + 1)]

        def agreement(c, b, t):
            cols = slice(P * t, P * (t + 1))
            return y1[c], w2_q[b][0][:, cols].bitcast(FP8X4), w2_q[b][1][:, cols]

        def products(c, b, z_codes, z_scales, kinds):
            width = CHUNKS[c][1] - CHUNKS[c][0]
            per_bank = BANK // width
            for kind in kinds:
                for t in range(PACK):
                    banks, codes, scales = kind(c, b, t)
                    place = t % per_bank
                    nc.tensor.matmul_mx(
                        out=banks[t // per_bank][:, width * place : width * (place + 1)],
                        lhsT=codes,
                        lhsT_scale=scales,
                        rhs=z_codes.bitcast(FP8X4),
                        rhs_scale=z_scales,
                        start=(b == 0 and place == 0),
                        stop=(b == 1 and place == per_bank - 1),
                    )

        for kind in (level, agreement):
            for c, (m0, m1) in enumerate(CHUNKS):
                products(c, 0, z0_q[0][:, m0:m1], z0_q[1][:, m0:m1], (kind,))

        out_rows = out.rearrange("(t p) m -> p t m", p=P)

        def pieces(c):
            width = CHUNKS[c][1] - CHUNKS[c][0]
            per_bank = BANK // width
            tiles = 2 if c == LAST else per_bank
            return [
                (t // per_bank, slice(width * (t % per_bank), width * (t % per_bank + tiles)), t, t + tiles)
                for t in range(0, PACK, tiles)
            ]

        def inverse_root(c, e, cols, tag=None):
            size = held("size%d_%d" % (c, e * BANK + cols.start), [P, cols.stop - cols.start], F32, tag=tag)
            root = ring.tile([P, cols.stop - cols.start], F32, name="root")
            nc.scalar.activation(size[:], y2[c][e][:, cols], ACT.Abs)
            nc.scalar.activation(root[:], size[:], ACT.Abs_reciprocal_sqrt, bias=1.0)
            return root

        def inverses(c, roots):
            done = []
            for e, cols, t0, t1 in pieces(c):
                root = roots[e] if e < len(roots) else inverse_root(c, e, cols)
                inverse = ring.tile([P, cols.stop - cols.start], F32, name="inverse")
                nc.scalar.activation(inverse[:], root[:], ACT.Square)
                done.append(inverse)
            return done

        def store(c, t0, t1, result):
            m0, m1 = CHUNKS[c]
            nc.sync.dma_start(out_rows[:, t0:t1, m0:m1], result.rearrange("p (t m) -> p t m", m=m1 - m0))

        inverse_of = []
        tags = [
            ("w1_rounded1", "z_rounded0"),
            ("z_rounded0", "z1_rounded0"),
            ("z1_rounded0", "z1_rounded1"),
        ]
        for c, (m0, m1) in enumerate(CHUNKS):
            z1 = pick_z(1, m0, m1, "z1_%d" % c, tags[c])
            copy = nc.vector.tensor_copy if c == LAST else nc.scalar.copy
            rounded = interleave("z1_rounded%d" % c, z1, copy)
            if c == 0:
                unread = held("unread", [P, 1], F32)
                nc.scalar.activation(unread[:], z1[:, PACK - 1, 0:1], ACT.Abs_reciprocal_sqrt, bias=1.0, scale=0.0)
            codes, scales = quantize_tile("z1_%d" % c, rounded)
            products(c, 1, codes[:], scales[:], (level, agreement))
            if c == 0:
                early = [inverse_root(0, 0, pieces(0)[0][1], "z1_rounded1")]
            else:
                inverse_of.append(inverses(c - 1, early if c == 1 else []))

        for c in range(LAST):
            m0, m1 = CHUNKS[c]
            result = held("result%d" % c, [P, PACK * (m1 - m0)], F32, tag="z1_rounded%d" % LAST if c == 0 else None)
            for (e, cols, t0, t1), inverse in zip(pieces(c), inverse_of[c]):
                part = result[:, (m1 - m0) * t0 : (m1 - m0) * t1]
                nc.vector.tensor_tensor(part, y1[c][e][:, cols], inverse[:], MULT)
                store(c, t0, t1, part)
        for e, cols, t0, t1 in pieces(LAST):
            root = inverse_root(LAST, e, cols)
            once = ring.tile([P, cols.stop - cols.start], F32, name="once")
            twice = ring.tile([P, cols.stop - cols.start], F32, name="twice")
            nc.vector.tensor_tensor(once[:], y1[LAST][e][:, cols], root[:], MULT)
            nc.vector.tensor_tensor(twice[:], once[:], root[:], MULT)
            store(LAST, t0, t1, twice[:])
